import numpy as np
import ml_dtypes


def mxq(x, axis, fmt="e4m3"):
    dtype, down = {"e4m3": (ml_dtypes.float8_e4m3fn, 7), "e5m2": (ml_dtypes.float8_e5m2, 14)}[fmt]
    v = np.moveaxis(np.asarray(x, np.float32).astype(ml_dtypes.bfloat16).astype(np.float64), axis, -1)
    blocks = v.reshape(v.shape[:-1] + (-1, 32))
    amax = np.abs(blocks).max(-1, keepdims=True)
    byte = np.maximum(np.where(amax > 0, np.frexp(amax)[1] - 1 + 127, 0) - down, 1)
    scale = np.exp2(byte - 127.0)
    codes = (blocks / scale).astype(np.float32).astype(dtype).astype(np.float64)
    return np.moveaxis((codes * scale).reshape(v.shape), -1, axis)


WIDE = False


def mx_kscale(k):
    if not WIDE:
        return np.ones(k)
    levels = np.array([10, -10, 5, -5, 0])
    if k % 512:
        return np.exp2(np.random.permutation(np.resize(levels, k // 32))).repeat(32)
    a = np.empty((k // 512, 16))
    for p in range(k // 512):
        a[p, :8] = np.random.permutation(np.resize(levels, 8))
        for g in range(8):
            far = levels[np.abs(levels - a[p, g]) >= 10]
            a[p, g + 8] = far[np.random.randint(len(far))]
    return np.exp2(a.ravel()).repeat(32)


def f64(x):
    return np.asarray(x).astype(np.float64)


def striped(idx):
    return np.tile(idx.reshape(-1, 16).T, (8, 1)).astype(np.uint16)


def unstriped(offs):
    return offs[:16].T.reshape(-1).astype(np.int64)


K, T, E, C, N = 512, 1024, 2, 512, 512


def setup_inputs():
    n = np.random.standard_normal
    idx = np.random.permutation(T)[:E * C]
    s = mx_kscale(E * C)[None, :]
    xT = n((K, T)); dyT = n((N, T))
    xT[:, idx] *= s; dyT[:, idx] /= s
    return {
        "xT": xT.astype(np.float32),
        "dyT": dyT.astype(np.float32),
        "gate": np.tile(np.random.uniform(0.2, 1.0, E * C), (N, 1)).astype(np.float32),
        "offs": striped(idx),
    }


def reference(xT, dyT, gate, offs):
    idx = unstriped(offs)
    xq = mxq(f64(xT)[:, idx], 1, "e4m3")
    gq = mxq(f64(gate) * f64(dyT)[:, idx], 1, "e4m3")
    return np.stack([(xq[:, e * C:(e + 1) * C] @ gq[:, e * C:(e + 1) * C].T) for e in range(E)])

@@ -1,0 +1,165 @@
+from contextlib import ExitStack
+
+import concourse.mybir as mybir
+from concourse.masks import make_identity
+
+K, T, E, C, N = 512, 1024, 2, 512, 512
+FLOPS = 2 * E * C * K * N
+BYTES = 4 * (K * T + N * T + T + E * K * N) + 2 * 128 * (E * C // 16)
+
+F32 = mybir.dt.float32
+BF16 = mybir.dt.bfloat16
+U32 = mybir.dt.uint32
+U16 = mybir.dt.uint16
+U8 = mybir.dt.uint8
+FP8X4 = mybir.dt.float8_e4m3fn_x4
+MULT = mybir.AluOpType.mult
+
+P = 128
+PACK = 4
+
+
+def tile_moe_bdw_lin_none_kernel(tc, xT, dyT, gate, offs, out):
+    nc = tc.nc
+    with ExitStack() as ctx:
+        keep = ctx.enter_context(tc.tile_pool(name="keep", bufs=1))
+        psum = ctx.enter_context(tc.psum_pool(name="psum", bufs=1))
+
+        offsets = keep.tile([P, E * C // 16], U16, name="offsets")
+        nc.sync.dma_start(offsets[:], offs)
+        gate_sb = [keep.tile([P, C], F32, name=f"gate{e}") for e in range(E)]
+        dy = [keep.tile([P, T], F32, name=f"dy{b}") for b in range(4)]
+        x = [keep.tile([P, 2, T], F32, name=f"x{h}") for h in range(2)]
+        xp = [keep.tile([P, 2 * T], BF16, name=f"xp{h}") for h in range(2)]
+
+        def load_gate(e):
+            nc.sync.dma_start(gate_sb[e][:], gate[0:P, e * C : (e + 1) * C])
+
+        def load_dy(b):
+            nc.sync.dma_start(dy[b][:], dyT[b * P : (b + 1) * P, :])
+
+        def load_x(h):
+            nc.sync.dma_start(x[h][:], xT[h * 256 : (h + 1) * 256, :].rearrange("(q e) w -> q e w", e=2))
+
+        load_gate(0)
+        load_dy(0)
+        load_gate(1)
+        load_dy(1)
+        load_x(0)
+        load_dy(2)
+        load_x(1)
+        load_dy(3)
+
+        ident = keep.tile([P, P], F32, name="ident")
+        make_identity(nc, ident[:])
+
+        def cast(h, part):
+            w = slice(512 * part, 512 * (part + 1))
+            nc.scalar.copy(
+                out=xp[h][:].rearrange("q (w e) -> q w e", e=2)[:, w, :],
+                in_=x[h][:, :, w].rearrange("q e w -> q w e"),
+            )
+
+        g_codes = [keep.tile([P, N], U32, name=f"gcodes{e}", align_bytes=64) for e in range(E)]
+        g_scales = [keep.tile([P, N], U8, name=f"gscales{e}", align_bytes=64) for e in range(E)]
+        x_codes = {}
+        x_scales = {}
+        gathered = {}
+        grouped = {}
+        state = {"bank": 0, "obank": 0}
+
+        def offsets_of(e):
+            return offsets[:, e * 32 : (e + 1) * 32]
+
+        def gather(u):
+            kind, b, e = u
+            if kind == "D":
+                g = keep.tile([P, C], F32, name=f"g{b}_{e}")
+                nc.vector.tensor_tensor(g[:], dy[b][:].indirect(offsets_of(e)), gate_sb[e][:], MULT)
+            else:
+                g = keep.tile([P, 2 * C], BF16, name=f"gx{b}_{e}")
+                nc.vector.tensor_copy(
+                    g[:].bitcast(U32).rearrange("q (t p) -> q p t", t=PACK),
+                    xp[b][:].bitcast(U32).indirect(offsets_of(e)),
+                )
+            gathered[u] = g
+
+        def turn(u):
+            kind, b, e = u
+            g = gathered[u]
+            bank = psum.tile([P, PACK, P], F32, name=f"turn{state['bank'] % 4}")
+            state["bank"] += 1
+            for t in range(PACK):
+                if kind == "D":
+                    src = g[:, t::PACK]
+                else:
+                    src = g[:].bitcast(F32)[:, t * P : (t + 1) * P]
+                nc.tensor.transpose(bank[:, t, :], src, ident[:])
+            if kind == "D":
+                gr = keep.tile([P, P, PACK], BF16, name=f"gr{b}_{e}", align_bytes=64)
+                nc.scalar.copy(out=gr[:], in_=bank[:].rearrange("p t k -> p k t"))
+            else:
+                gr = keep.tile([P, 2 * P, PACK], BF16, name=f"grx{b}_{e}", align_bytes=64)
+                nc.scalar.copy(out=gr[:], in_=bank[:].bitcast(BF16).rearrange("p t k -> p k t"))
+            grouped[u] = gr
+
+        def quantize(u):
+            kind, b, e = u
+            src = grouped[u][:].rearrange("p k t -> p (k t)")
+            if kind == "D":
+                cols = slice(b * P, (b + 1) * P)
+                nc.vector.quantize_mx(
+                    out=g_codes[e][:, cols].bitcast(FP8X4), scales=g_scales[e][:, cols], in_=src
+                )
+            else:
+                xc = keep.tile([P, 2 * P], U32, name=f"xcodes{b}_{e}", align_bytes=64)
+                xs = keep.tile([P, 2 * P], U8, name=f"xscales{b}_{e}", align_bytes=64)
+                nc.vector.quantize_mx(out=xc[:].bitcast(FP8X4), scales=xs[:], in_=src)
+                x_codes[b, e] = xc
+                x_scales[b, e] = xs
+
+        def multiply(e, h):
+            for c in range(2):
+                cols = slice(c * P, (c + 1) * P)
+                acc = psum.tile([P, N], F32, name=f"acc{state['obank'] % 4}")
+                state["obank"] += 1
+                nc.tensor.matmul_mx(
+                    out=acc[:],
+                    lhsT=x_codes[h, e][:, cols].bitcast(FP8X4),
+                    lhsT_scale=x_scales[h, e][:, cols],
+                    rhs=g_codes[e][:].bitcast(FP8X4),
+                    rhs_scale=g_scales[e][:],
+                    start=True,
+                    stop=True,
+                )
+                res = keep.tile([P, N], F32, name=f"res{e}_{h}_{c}")
+                if e == 0 or c == 0:
+                    nc.scalar.copy(out=res[:], in_=acc[:])
+                else:
+                    nc.vector.tensor_copy(out=res[:], in_=acc[:])
+                k0 = h * 256 + c * P
+                nc.sync.dma_start(out[e, k0 : k0 + P, :], res[:])
+
+        units = [
+            ("D", 0, 0), ("D", 0, 1), ("D", 1, 0), ("D", 1, 1),
+            ("D", 2, 0), ("X", 0, 0), ("D", 2, 1), ("D", 3, 0),
+            ("D", 3, 1), ("X", 1, 0), ("X", 0, 1), ("X", 1, 1),
+        ]
+        casts = {3: (0, 0), 4: (0, 1), 6: (1, 0), 7: (1, 1)}
+        done = set()
+        multiplied = set()
+        for i in range(len(units) + 3):
+            if i in casts:
+                cast(*casts[i])
+            if i < len(units):
+                gather(units[i])
+            if 0 <= i - 1 < len(units):
+                turn(units[i - 1])
+            if 0 <= i - 3:
+                quantize(units[i - 3])
+                done.add(units[i - 3])
+                for e in range(E):
+                    for h in range(2):
+                        if (e, h) not in multiplied and ("X", h, e) in done and all(("D", b, e) in done for b in range(4)):
+                            multiplied.add((e, h))
+                            multiply(e, h)

@@ -14,9 +14,17 @@ U16 = mybir.dt.uint16
 U8 = mybir.dt.uint8
 FP8X4 = mybir.dt.float8_e4m3fn_x4
 MULT = mybir.AluOpType.mult
+COPY = mybir.ActivationFunctionType.Copy
 
 P = 128
 PACK = 4
+UNITS = [('D', 2, 1), ('D', 3, 0), ('D', 1, 1), ('X', 0, 1), ('D', 2, 0), ('D', 0, 1), ('X', 3, 1), ('D', 3, 1), ('D', 0, 0), ('D', 1, 0), ('X', 2, 0), ('X', 2, 1), ('X', 1, 1), ('X', 3, 0), ('X', 1, 0), ('X', 0, 0)]
+CAST_AT = [3, 4, 1, 4]
+X_ROAD = "VVVV"
+COPY_ON_VECTOR = ('X21', 'X20', 'X00', 'X10', 'X11', 'D10', 'X30')
+RES = "VVSSSSSS"
+LAG_Q, LAG_O = 1, 1
+LOADS = "x0 g1 d3 x3 g0 d1 d2 x2 x1 d0"
 
 
 def tile_moe_bdw_lin_none_kernel(tc, xT, dyT, gate, offs, out):
@@ -27,43 +35,39 @@ def tile_moe_bdw_lin_none_kernel(tc, xT, dyT, gate, offs, out):
 
         offsets = keep.tile([P, E * C // 16], U16, name="offsets")
         nc.sync.dma_start(offsets[:], offs)
-        gate_sb = [keep.tile([P, C], F32, name=f"gate{e}") for e in range(E)]
-        dy = [keep.tile([P, T], F32, name=f"dy{b}") for b in range(4)]
-        x = [keep.tile([P, 2, T], F32, name=f"x{h}") for h in range(2)]
-        xp = [keep.tile([P, 2 * T], BF16, name=f"xp{h}") for h in range(2)]
-
-        def load_gate(e):
-            nc.sync.dma_start(gate_sb[e][:], gate[0:P, e * C : (e + 1) * C])
-
-        def load_dy(b):
-            nc.sync.dma_start(dy[b][:], dyT[b * P : (b + 1) * P, :])
-
-        def load_x(h):
-            nc.sync.dma_start(x[h][:], xT[h * 256 : (h + 1) * 256, :].rearrange("(q e) w -> q e w", e=2))
-
-        load_gate(0)
-        load_dy(0)
-        load_gate(1)
-        load_dy(1)
-        load_x(0)
-        load_dy(2)
-        load_x(1)
-        load_dy(3)
+        gate_sb = {}
+        dy = {}
+        x = {}
+        for name in LOADS.split():
+            b = int(name[1])
+            if name[0] == "g":
+                gate_sb[b] = keep.tile([P, C], F32, name=f"gate{b}")
+                nc.sync.dma_start(gate_sb[b][:], gate[0:P, b * C : (b + 1) * C])
+            elif name[0] == "d":
+                dy[b] = keep.tile([P, T], F32, name=f"dy{b}")
+                nc.sync.dma_start(dy[b][:], dyT[b * P : (b + 1) * P, :])
+            else:
+                x[b] = keep.tile([P, T], F32, name=f"x{b}")
+                nc.sync.dma_start(x[b][:], xT[b * P : (b + 1) * P, :])
 
         ident = keep.tile([P, P], F32, name="ident")
         make_identity(nc, ident[:])
 
-        def cast(h, part):
-            w = slice(512 * part, 512 * (part + 1))
-            nc.scalar.copy(
-                out=xp[h][:].rearrange("q (w e) -> q w e", e=2)[:, w, :],
-                in_=x[h][:, :, w].rearrange("q e w -> q w e"),
-            )
+        x_bf = {}
+
+        def cast(b):
+            x_bf[b] = keep.tile([P, T], BF16, name=f"xbf{b}")
+            if X_ROAD[b] == "V":
+                nc.vector.tensor_copy(x_bf[b][:], x[b][:])
+            elif X_ROAD[b] == "S":
+                nc.scalar.copy(out=x_bf[b][:], in_=x[b][:])
+            else:
+                nc.gpsimd.tensor_copy(x_bf[b][:], x[b][:])
 
         g_codes = [keep.tile([P, N], U32, name=f"gcodes{e}", align_bytes=64) for e in range(E)]
         g_scales = [keep.tile([P, N], U8, name=f"gscales{e}", align_bytes=64) for e in range(E)]
-        x_codes = {}
-        x_scales = {}
+        x_codes = [keep.tile([P, K], U32, name=f"xcodes{e}", align_bytes=64) for e in range(E)]
+        x_scales = [keep.tile([P, K], U8, name=f"xscales{e}", align_bytes=64) for e in range(E)]
         gathered = {}
         grouped = {}
         state = {"bank": 0, "obank": 0}
@@ -77,11 +81,12 @@ def tile_moe_bdw_lin_none_kernel(tc, xT, dyT, gate, offs, out):
                 g = keep.tile([P, C], F32, name=f"g{b}_{e}")
                 nc.vector.tensor_tensor(g[:], dy[b][:].indirect(offsets_of(e)), gate_sb[e][:], MULT)
             else:
-                g = keep.tile([P, 2 * C], BF16, name=f"gx{b}_{e}")
-                nc.vector.tensor_copy(
-                    g[:].bitcast(U32).rearrange("q (t p) -> q p t", t=PACK),
-                    xp[b][:].bitcast(U32).indirect(offsets_of(e)),
-                )
+                g = keep.tile([P, C], BF16, name=f"gx{b}_{e}")
+                view = g[:].rearrange("q (u p s) -> q p u s", u=2, s=2)
+                if X_ROAD[b] == "B":
+                    nc.vector.tensor_copy(view, x[b][:].indirect(offsets_of(e)))
+                else:
+                    nc.scalar.activation(view, x_bf[b][:].indirect(offsets_of(e)), COPY)
             gathered[u] = g
 
         def turn(u):
@@ -89,77 +94,83 @@ def tile_moe_bdw_lin_none_kernel(tc, xT, dyT, gate, offs, out):
             g = gathered[u]
             bank = psum.tile([P, PACK, P], F32, name=f"turn{state['bank'] % 4}")
             state["bank"] += 1
-            for t in range(PACK):
-                if kind == "D":
-                    src = g[:, t::PACK]
-                else:
-                    src = g[:].bitcast(F32)[:, t * P : (t + 1) * P]
-                nc.tensor.transpose(bank[:, t, :], src, ident[:])
+            gr = keep.tile([P, P * PACK], BF16, name=f"gr{kind}{b}_{e}", align_bytes=64)
             if kind == "D":
-                gr = keep.tile([P, P, PACK], BF16, name=f"gr{b}_{e}", align_bytes=64)
-                nc.scalar.copy(out=gr[:], in_=bank[:].rearrange("p t k -> p k t"))
+                for t in range(PACK):
+                    nc.tensor.transpose(bank[:, t, :], g[:, t::PACK], ident[:])
+                dst = gr[:].rearrange("p (k t) -> p k t", t=PACK)
+                src = bank[:].rearrange("p t k -> p k t")
             else:
-                gr = keep.tile([P, 2 * P, PACK], BF16, name=f"grx{b}_{e}", align_bytes=64)
-                nc.scalar.copy(out=gr[:], in_=bank[:].bitcast(BF16).rearrange("p t k -> p k t"))
+                for h in range(2):
+                    nc.tensor.transpose(bank[:, h, :], g[:].bitcast(F32)[:, h * P : (h + 1) * P], ident[:])
+                dst = gr[:].bitcast(F32).rearrange("p (k u) -> p k u", u=2)
+                src = bank[:, 0:2, :].rearrange("p u k -> p k u")
+            if f"{kind}{b}{e}" in COPY_ON_VECTOR:
+                nc.vector.tensor_copy(dst, src)
+            else:
+                nc.scalar.copy(out=dst, in_=src)
             grouped[u] = gr
 
         def quantize(u):
             kind, b, e = u
-            src = grouped[u][:].rearrange("p k t -> p (k t)")
-            if kind == "D":
-                cols = slice(b * P, (b + 1) * P)
-                nc.vector.quantize_mx(
-                    out=g_codes[e][:, cols].bitcast(FP8X4), scales=g_scales[e][:, cols], in_=src
-                )
-            else:
-                xc = keep.tile([P, 2 * P], U32, name=f"xcodes{b}_{e}", align_bytes=64)
-                xs = keep.tile([P, 2 * P], U8, name=f"xscales{b}_{e}", align_bytes=64)
-                nc.vector.quantize_mx(out=xc[:].bitcast(FP8X4), scales=xs[:], in_=src)
-                x_codes[b, e] = xc
-                x_scales[b, e] = xs
+            cols = slice(b * P, (b + 1) * P)
+            codes, scales = (g_codes, g_scales) if kind == "D" else (x_codes, x_scales)
+            nc.vector.quantize_mx(
+                out=codes[e][:, cols].bitcast(FP8X4), scales=scales[e][:, cols], in_=grouped[u][:]
+            )
 
-        def multiply(e, h):
-            for c in range(2):
-                cols = slice(c * P, (c + 1) * P)
-                acc = psum.tile([P, N], F32, name=f"acc{state['obank'] % 4}")
-                state["obank"] += 1
-                nc.tensor.matmul_mx(
-                    out=acc[:],
-                    lhsT=x_codes[h, e][:, cols].bitcast(FP8X4),
-                    lhsT_scale=x_scales[h, e][:, cols],
-                    rhs=g_codes[e][:].bitcast(FP8X4),
-                    rhs_scale=g_scales[e][:],
-                    start=True,
-                    stop=True,
-                )
-                res = keep.tile([P, N], F32, name=f"res{e}_{h}_{c}")
-                if e == 0 or c == 0:
-                    nc.scalar.copy(out=res[:], in_=acc[:])
+        def multiply(e, b, n0, width, engine):
+            acc = psum.tile([P, N], F32, name=f"acc{state['obank'] % 4}")
+            state["obank"] += 1
+            k = slice(b * P, (b + 1) * P)
+            n = slice(n0, n0 + width)
+            nc.tensor.matmul_mx(
+                out=acc[:, 0:width],
+                lhsT=x_codes[e][:, k].bitcast(FP8X4),
+                lhsT_scale=x_scales[e][:, k],
+                rhs=g_codes[e][:, n].bitcast(FP8X4),
+                rhs_scale=g_scales[e][:, n],
+                start=True,
+                stop=True,
+            )
+
+            def leave():
+                res = keep.tile([P, width], F32, name=f"res{e}_{b}_{n0}")
+                if engine == "S":
+                    nc.scalar.copy(out=res[:], in_=acc[:, 0:width])
                 else:
-                    nc.vector.tensor_copy(out=res[:], in_=acc[:])
-                k0 = h * 256 + c * P
-                nc.sync.dma_start(out[e, k0 : k0 + P, :], res[:])
+                    nc.vector.tensor_copy(out=res[:], in_=acc[:, 0:width])
+                nc.sync.dma_start(out[e, k, n], res[:])
 
-        units = [
-            ("D", 0, 0), ("D", 0, 1), ("D", 1, 0), ("D", 1, 1),
-            ("D", 2, 0), ("X", 0, 0), ("D", 2, 1), ("D", 3, 0),
-            ("D", 3, 1), ("X", 1, 0), ("X", 0, 1), ("X", 1, 1),
-        ]
-        casts = {3: (0, 0), 4: (0, 1), 6: (1, 0), 7: (1, 1)}
+            return leave
+
         done = set()
-        multiplied = set()
-        for i in range(len(units) + 3):
-            if i in casts:
-                cast(*casts[i])
-            if i < len(units):
-                gather(units[i])
-            if 0 <= i - 1 < len(units):
-                turn(units[i - 1])
-            if 0 <= i - 3:
-                quantize(units[i - 3])
-                done.add(units[i - 3])
-                for e in range(E):
-                    for h in range(2):
-                        if (e, h) not in multiplied and ("X", h, e) in done and all(("D", b, e) in done for b in range(4)):
-                            multiplied.add((e, h))
-                            multiply(e, h)
+        issued = set()
+        pending = []
+        for i in range(len(UNITS) + LAG_Q + LAG_O + 1):
+            for b in range(4):
+                if X_ROAD[b] != "B" and CAST_AT[b] == i:
+                    cast(b)
+            if i < len(UNITS):
+                gather(UNITS[i])
+            if 0 <= i - 1 < len(UNITS):
+                turn(UNITS[i - 1])
+            for at, leave in [p for p in pending if p[0] == i]:
+                leave()
+            if 0 <= i - LAG_Q < len(UNITS):
+                quantize(UNITS[i - LAG_Q])
+                done.add(UNITS[i - LAG_Q])
+            for e in range(E):
+                for b in range(4):
+                    need = [("X", b, e)] + [("D", j, e) for j in range(4)]
+                    if (e, b) not in issued and all(v in done for v in need):
+                        issued.add((e, b))
+                        if need[0] == UNITS[-1]:
+                            leaves = [multiply(e, b, 256 * j, 256, "SV"[j]) for j in range(2)]
+                        else:
+                            leaves = [multiply(e, b, 0, N, RES[e * 4 + b])]
+                        if LAG_O == 0:
+                            for leave in leaves:
+                                leave()
+                        else:
+                            pending.extend([(i + LAG_O, leave) for leave in leaves])

@@ -14,17 +14,17 @@ U16 = mybir.dt.uint16
 U8 = mybir.dt.uint8
 FP8X4 = mybir.dt.float8_e4m3fn_x4
 MULT = mybir.AluOpType.mult
+ADD = mybir.AluOpType.add
 COPY = mybir.ActivationFunctionType.Copy
 
 P = 128
 PACK = 4
-UNITS = [('D', 2, 1), ('D', 3, 0), ('D', 1, 1), ('X', 0, 1), ('D', 2, 0), ('D', 0, 1), ('X', 3, 1), ('D', 3, 1), ('D', 0, 0), ('D', 1, 0), ('X', 2, 0), ('X', 2, 1), ('X', 1, 1), ('X', 3, 0), ('X', 1, 0), ('X', 0, 0)]
-CAST_AT = [3, 4, 1, 4]
-X_ROAD = "VVVV"
-COPY_ON_VECTOR = ('X21', 'X20', 'X00', 'X10', 'X11', 'D10', 'X30')
-RES = "VVSSSSSS"
-LAG_Q, LAG_O = 1, 1
-LOADS = "x0 g1 d3 x3 g0 d1 d2 x2 x1 d0"
+D_UNITS = [(0, 1), (0, 0), (3, 0), (2, 0), (1, 0), (2, 1), (3, 1), (1, 1)]
+X_UNITS = [(2, 0), (1, 0), (3, 0), (0, 0), (0, 1), (3, 1), (2, 1), (1, 1)]
+COPY_X = "SSSSSSSV"
+RES = "SSSSSSVV"
+LAG_QD, LAG_QX, LAG_X, LAG_O = 1, 3, 1, 2
+LOADS = "d0 g0 x1 d3 x2 d2 x3 d1 x0"
 
 
 def tile_moe_bdw_lin_none_kernel(tc, xT, dyT, gate, offs, out):
@@ -35,14 +35,13 @@ def tile_moe_bdw_lin_none_kernel(tc, xT, dyT, gate, offs, out):
 
         offsets = keep.tile([P, E * C // 16], U16, name="offsets")
         nc.sync.dma_start(offsets[:], offs)
-        gate_sb = {}
         dy = {}
         x = {}
         for name in LOADS.split():
             b = int(name[1])
             if name[0] == "g":
-                gate_sb[b] = keep.tile([P, C], F32, name=f"gate{b}")
-                nc.sync.dma_start(gate_sb[b][:], gate[0:P, b * C : (b + 1) * C])
+                gate_sb = keep.tile([P, E, PACK], F32, name="gate_sb")
+                nc.sync.dma_start(gate_sb[:], gate[0:1, :].rearrange("o (e p t) -> p (o e) t", e=E, t=PACK))
             elif name[0] == "d":
                 dy[b] = keep.tile([P, T], F32, name=f"dy{b}")
                 nc.sync.dma_start(dy[b][:], dyT[b * P : (b + 1) * P, :])
@@ -57,12 +56,7 @@ def tile_moe_bdw_lin_none_kernel(tc, xT, dyT, gate, offs, out):
 
         def cast(b):
             x_bf[b] = keep.tile([P, T], BF16, name=f"xbf{b}")
-            if X_ROAD[b] == "V":
-                nc.vector.tensor_copy(x_bf[b][:], x[b][:])
-            elif X_ROAD[b] == "S":
-                nc.scalar.copy(out=x_bf[b][:], in_=x[b][:])
-            else:
-                nc.gpsimd.tensor_copy(x_bf[b][:], x[b][:])
+            nc.gpsimd.tensor_scalar(x_bf[b][:], x[b][:], 1.0, 0.0, MULT, ADD)
 
         g_codes = [keep.tile([P, N], U32, name=f"gcodes{e}", align_bytes=64) for e in range(E)]
         g_scales = [keep.tile([P, N], U8, name=f"gscales{e}", align_bytes=64) for e in range(E)]
@@ -70,58 +64,64 @@ def tile_moe_bdw_lin_none_kernel(tc, xT, dyT, gate, offs, out):
         x_scales = [keep.tile([P, K], U8, name=f"xscales{e}", align_bytes=64) for e in range(E)]
         gathered = {}
         grouped = {}
-        state = {"bank": 0, "obank": 0}
+        count = {"acc": 0}
 
         def offsets_of(e):
             return offsets[:, e * 32 : (e + 1) * 32]
 
-        def gather(u):
-            kind, b, e = u
-            if kind == "D":
-                g = keep.tile([P, C], F32, name=f"g{b}_{e}")
-                nc.vector.tensor_tensor(g[:], dy[b][:].indirect(offsets_of(e)), gate_sb[e][:], MULT)
-            else:
-                g = keep.tile([P, C], BF16, name=f"gx{b}_{e}")
-                view = g[:].rearrange("q (u p s) -> q p u s", u=2, s=2)
-                if X_ROAD[b] == "B":
-                    nc.vector.tensor_copy(view, x[b][:].indirect(offsets_of(e)))
-                else:
-                    nc.scalar.activation(view, x_bf[b][:].indirect(offsets_of(e)), COPY)
-            gathered[u] = g
+        def ring(name, i, size):
+            return f"{name}{i % size if size else i}"
 
-        def turn(u):
-            kind, b, e = u
-            g = gathered[u]
-            bank = psum.tile([P, PACK, P], F32, name=f"turn{state['bank'] % 4}")
-            state["bank"] += 1
-            gr = keep.tile([P, P * PACK], BF16, name=f"gr{kind}{b}_{e}", align_bytes=64)
-            if kind == "D":
-                for t in range(PACK):
-                    nc.tensor.transpose(bank[:, t, :], g[:, t::PACK], ident[:])
-                dst = gr[:].rearrange("p (k t) -> p k t", t=PACK)
-                src = bank[:].rearrange("p t k -> p k t")
-            else:
-                for h in range(2):
-                    nc.tensor.transpose(bank[:, h, :], g[:].bitcast(F32)[:, h * P : (h + 1) * P], ident[:])
-                dst = gr[:].bitcast(F32).rearrange("p (k u) -> p k u", u=2)
-                src = bank[:, 0:2, :].rearrange("p u k -> p k u")
-            if f"{kind}{b}{e}" in COPY_ON_VECTOR:
+        def gather_d(i):
+            b, e = D_UNITS[i]
+            g = keep.tile([P, C], F32, name=ring("gd", i, 3))
+            nc.vector.tensor_copy(g[:], dy[b][:].indirect(offsets_of(e)))
+            gathered["D", i] = g
+
+        def gather_x(i):
+            b, e = X_UNITS[i]
+            g = keep.tile([P, C], BF16, name=ring("gx", i, 0))
+            view = g[:].rearrange("q (u p s) -> q p u s", u=2, s=2)
+            nc.scalar.activation(view, x_bf[b][:].indirect(offsets_of(e)), COPY)
+            gathered["X", i] = g
+
+        def turn_d(i):
+            b, e = D_UNITS[i]
+            g = gathered["D", i]
+            bank = psum.tile([P, PACK, P], F32, name=ring("turnd", i, 2))
+            for t in range(PACK):
+                nc.tensor.transpose(bank[:, t, :], g[:, t::PACK], ident[:])
+            gr = keep.tile([P, P, PACK], BF16, name=ring("grd", i, 2), align_bytes=64)
+            nc.vector.tensor_tensor(
+                gr[:], bank[:].rearrange("p t k -> p k t"), gate_sb[:, e : e + 1, :].to_broadcast([P, P, PACK]), MULT
+            )
+            grouped["D", i] = gr[:].rearrange("p k t -> p (k t)")
+
+        def turn_x(i):
+            g = gathered["X", i]
+            bank = psum.tile([P, 2, P], F32, name=ring("turnx", i, 3))
+            for h in range(2):
+                nc.tensor.transpose(bank[:, h, :], g[:].bitcast(F32)[:, h * P : (h + 1) * P], ident[:])
+            gr = keep.tile([P, P * PACK], BF16, name=ring("grx", i, 0), align_bytes=64)
+            dst = gr[:].bitcast(F32).rearrange("p (k u) -> p k u", u=2)
+            src = bank[:].rearrange("p u k -> p k u")
+            if COPY_X[i] == "V":
                 nc.vector.tensor_copy(dst, src)
             else:
                 nc.scalar.copy(out=dst, in_=src)
-            grouped[u] = gr
+            grouped["X", i] = gr[:]
 
-        def quantize(u):
-            kind, b, e = u
+        def quantize(kind, i):
+            b, e = (D_UNITS if kind == "D" else X_UNITS)[i]
             cols = slice(b * P, (b + 1) * P)
             codes, scales = (g_codes, g_scales) if kind == "D" else (x_codes, x_scales)
             nc.vector.quantize_mx(
-                out=codes[e][:, cols].bitcast(FP8X4), scales=scales[e][:, cols], in_=grouped[u][:]
+                out=codes[e][:, cols].bitcast(FP8X4), scales=scales[e][:, cols], in_=grouped[kind, i]
             )
 
         def multiply(e, b, n0, width, engine):
-            acc = psum.tile([P, N], F32, name=f"acc{state['obank'] % 4}")
-            state["obank"] += 1
+            acc = psum.tile([P, N], F32, name=ring("acc", count["acc"], 3))
+            count["acc"] += 1
             k = slice(b * P, (b + 1) * P)
             n = slice(n0, n0 + width)
             nc.tensor.matmul_mx(
@@ -145,30 +145,40 @@ def tile_moe_bdw_lin_none_kernel(tc, xT, dyT, gate, offs, out):
             return leave
 
         done = set()
-        issued = set()
+        issued = []
         pending = []
-        for i in range(len(UNITS) + LAG_Q + LAG_O + 1):
-            for b in range(4):
-                if X_ROAD[b] != "B" and CAST_AT[b] == i:
-                    cast(b)
-            if i < len(UNITS):
-                gather(UNITS[i])
-            if 0 <= i - 1 < len(UNITS):
-                turn(UNITS[i - 1])
+        cast_done = set()
+        for i in range(8 + LAG_X + max(LAG_QD, LAG_QX) + LAG_O + 2):
+            ahead = i - LAG_X + 1
+            if 0 <= ahead < 8 and X_UNITS[ahead][0] not in cast_done:
+                cast_done.add(X_UNITS[ahead][0])
+                cast(X_UNITS[ahead][0])
+            if i < 8:
+                gather_d(i)
+            j = i - LAG_X
+            if 0 <= j < 8:
+                gather_x(j)
+            if 0 <= i - 1 < 8:
+                turn_d(i - 1)
+            if 0 <= j - 1 < 8:
+                turn_x(j - 1)
             for at, leave in [p for p in pending if p[0] == i]:
                 leave()
-            if 0 <= i - LAG_Q < len(UNITS):
-                quantize(UNITS[i - LAG_Q])
-                done.add(UNITS[i - LAG_Q])
+            if 0 <= i - LAG_QD < 8:
+                quantize("D", i - LAG_QD)
+                done.add(("D",) + D_UNITS[i - LAG_QD])
+            if 0 <= j - LAG_QX < 8:
+                quantize("X", j - LAG_QX)
+                done.add(("X",) + X_UNITS[j - LAG_QX])
             for e in range(E):
                 for b in range(4):
-                    need = [("X", b, e)] + [("D", j, e) for j in range(4)]
-                    if (e, b) not in issued and all(v in done for v in need):
-                        issued.add((e, b))
-                        if need[0] == UNITS[-1]:
-                            leaves = [multiply(e, b, 256 * j, 256, "SV"[j]) for j in range(2)]
+                    need = [("X", b, e)] + [("D", q, e) for q in range(4)]
+                    if (b, e) not in issued and all(v in done for v in need):
+                        issued.append((b, e))
+                        if (b, e) == X_UNITS[-1] and True:
+                            leaves = [multiply(e, b, 256 * q, 256, "SV"[q]) for q in range(2)]
                         else:
-                            leaves = [multiply(e, b, 0, N, RES[e * 4 + b])]
+                            leaves = [multiply(e, b, 0, N, RES[len(issued) - 1])]
                         if LAG_O == 0:
                             for leave in leaves:
                                 leave()

@@ -19,12 +19,14 @@ COPY = mybir.ActivationFunctionType.Copy
 
 P = 128
 PACK = 4
-D_UNITS = [(0, 1), (0, 0), (3, 0), (2, 0), (1, 0), (2, 1), (3, 1), (1, 1)]
-X_UNITS = [(2, 0), (1, 0), (3, 0), (0, 0), (0, 1), (3, 1), (2, 1), (1, 1)]
-COPY_X = "SSSSSSSV"
-RES = "SSSSSSVV"
-LAG_QD, LAG_QX, LAG_X, LAG_O = 1, 3, 1, 2
-LOADS = "d0 g0 x1 d3 x2 d2 x3 d1 x0"
+D_UNITS = [(2, 1), (1, 0), (2, 0), (3, 0), (0, 0), (0, 1), (3, 1), (1, 1)]
+X_UNITS = [(0, 0), (3, 0), (2, 0), (0, 1), (1, 1), (3, 1), (2, 1), (1, 0)]
+CAST_ON = "SGGG"
+CAST_AHEAD = 2
+COPY_X = "SSSSSSSS"
+RES = "SSSSVSSS"
+LAG_QD, LAG_QX, LAG_X, LAG_O = 2, 2, 3, 1
+LOADS = "d1 g0 x0 d2 x2 d3 x3 d0 x1"
 
 
 def tile_moe_bdw_lin_none_kernel(tc, xT, dyT, gate, offs, out):
@@ -56,7 +58,13 @@ def tile_moe_bdw_lin_none_kernel(tc, xT, dyT, gate, offs, out):
 
         def cast(b):
             x_bf[b] = keep.tile([P, T], BF16, name=f"xbf{b}")
-            nc.gpsimd.tensor_scalar(x_bf[b][:], x[b][:], 1.0, 0.0, MULT, ADD)
+            engine = CAST_ON[len(x_bf) - 1]
+            if engine == "S":
+                nc.scalar.copy(out=x_bf[b][:], in_=x[b][:])
+            elif engine == "V":
+                nc.vector.tensor_copy(x_bf[b][:], x[b][:])
+            else:
+                nc.gpsimd.tensor_scalar(x_bf[b][:], x[b][:], 1.0, 0.0, MULT, ADD)
 
         g_codes = [keep.tile([P, N], U32, name=f"gcodes{e}", align_bytes=64) for e in range(E)]
         g_scales = [keep.tile([P, N], U8, name=f"gscales{e}", align_bytes=64) for e in range(E)]
@@ -64,6 +72,9 @@ def tile_moe_bdw_lin_none_kernel(tc, xT, dyT, gate, offs, out):
         x_scales = [keep.tile([P, K], U8, name=f"xscales{e}", align_bytes=64) for e in range(E)]
         gathered = {}
         grouped = {}
+        pairs = {}
+        ready = {}
+        done = set()
         count = {"acc": 0}
 
         def offsets_of(e):
@@ -74,7 +85,7 @@ def tile_moe_bdw_lin_none_kernel(tc, xT, dyT, gate, offs, out):
 
         def gather_d(i):
             b, e = D_UNITS[i]
-            g = keep.tile([P, C], F32, name=ring("gd", i, 3))
+            g = keep.tile([P, C], F32, name=ring("gd", i, 0))
             nc.vector.tensor_copy(g[:], dy[b][:].indirect(offsets_of(e)))
             gathered["D", i] = g
 
@@ -88,18 +99,19 @@ def tile_moe_bdw_lin_none_kernel(tc, xT, dyT, gate, offs, out):
         def turn_d(i):
             b, e = D_UNITS[i]
             g = gathered["D", i]
-            bank = psum.tile([P, PACK, P], F32, name=ring("turnd", i, 2))
+            bank = psum.tile([P, PACK, P], F32, name=ring("turnd", i, 3))
             for t in range(PACK):
                 nc.tensor.transpose(bank[:, t, :], g[:, t::PACK], ident[:])
-            gr = keep.tile([P, P, PACK], BF16, name=ring("grd", i, 2), align_bytes=64)
+            if (b // 2, e) not in pairs:
+                pairs[b // 2, e] = keep.tile([P, 2, P, PACK], BF16, name=f"grd{b // 2}_{e}", align_bytes=64)
+            gr = pairs[b // 2, e][:, b % 2]
             nc.vector.tensor_tensor(
-                gr[:], bank[:].rearrange("p t k -> p k t"), gate_sb[:, e : e + 1, :].to_broadcast([P, P, PACK]), MULT
+                gr, bank[:].rearrange("p t k -> p k t"), gate_sb[:, e : e + 1, :].to_broadcast([P, P, PACK]), MULT
             )
-            grouped["D", i] = gr[:].rearrange("p k t -> p (k t)")
 
         def turn_x(i):
             g = gathered["X", i]
-            bank = psum.tile([P, 2, P], F32, name=ring("turnx", i, 3))
+            bank = psum.tile([P, 2, P], F32, name=ring("turnx", i, 2))
             for h in range(2):
                 nc.tensor.transpose(bank[:, h, :], g[:].bitcast(F32)[:, h * P : (h + 1) * P], ident[:])
             gr = keep.tile([P, P * PACK], BF16, name=ring("grx", i, 0), align_bytes=64)
@@ -111,13 +123,26 @@ def tile_moe_bdw_lin_none_kernel(tc, xT, dyT, gate, offs, out):
                 nc.scalar.copy(out=dst, in_=src)
             grouped["X", i] = gr[:]
 
-        def quantize(kind, i):
-            b, e = (D_UNITS if kind == "D" else X_UNITS)[i]
-            cols = slice(b * P, (b + 1) * P)
-            codes, scales = (g_codes, g_scales) if kind == "D" else (x_codes, x_scales)
+        def quantize_d(i):
+            b, e = D_UNITS[i]
+            if ready.setdefault((b // 2, e), b) == b:
+                return
+            cols = slice(b // 2 * 2 * P, (b // 2 + 1) * 2 * P)
             nc.vector.quantize_mx(
-                out=codes[e][:, cols].bitcast(FP8X4), scales=scales[e][:, cols], in_=grouped[kind, i]
+                out=g_codes[e][:, cols].bitcast(FP8X4),
+                scales=g_scales[e][:, cols],
+                in_=pairs[b // 2, e][:].rearrange("p h k t -> p (h k t)"),
             )
+            done.add(("D", b, e))
+            done.add(("D", b + 1 - 2 * (b % 2), e))
+
+        def quantize_x(i):
+            b, e = X_UNITS[i]
+            cols = slice(b * P, (b + 1) * P)
+            nc.vector.quantize_mx(
+                out=x_codes[e][:, cols].bitcast(FP8X4), scales=x_scales[e][:, cols], in_=grouped["X", i]
+            )
+            done.add(("X", b, e))
 
         def multiply(e, b, n0, width, engine):
             acc = psum.tile([P, N], F32, name=ring("acc", count["acc"], 3))
@@ -144,15 +169,12 @@ def tile_moe_bdw_lin_none_kernel(tc, xT, dyT, gate, offs, out):
 
             return leave
 
-        done = set()
         issued = []
         pending = []
-        cast_done = set()
         for i in range(8 + LAG_X + max(LAG_QD, LAG_QX) + LAG_O + 2):
-            ahead = i - LAG_X + 1
-            if 0 <= ahead < 8 and X_UNITS[ahead][0] not in cast_done:
-                cast_done.add(X_UNITS[ahead][0])
-                cast(X_UNITS[ahead][0])
+            for ahead in range(min(i - LAG_X + CAST_AHEAD + 1, 8)):
+                if X_UNITS[ahead][0] not in x_bf:
+                    cast(X_UNITS[ahead][0])
             if i < 8:
                 gather_d(i)
             j = i - LAG_X
@@ -165,11 +187,9 @@ def tile_moe_bdw_lin_none_kernel(tc, xT, dyT, gate, offs, out):
             for at, leave in [p for p in pending if p[0] == i]:
                 leave()
             if 0 <= i - LAG_QD < 8:
-                quantize("D", i - LAG_QD)
-                done.add(("D",) + D_UNITS[i - LAG_QD])
+                quantize_d(i - LAG_QD)
             if 0 <= j - LAG_QX < 8:
-                quantize("X", j - LAG_QX)
-                done.add(("X",) + X_UNITS[j - LAG_QX])
+                quantize_x(j - LAG_QX)
             for e in range(E):
                 for b in range(4):
                     need = [("X", b, e)] + [("D", q, e) for q in range(4)]

@@ -19,14 +19,14 @@ COPY = mybir.ActivationFunctionType.Copy
 
 P = 128
 PACK = 4
-D_UNITS = [(2, 1), (1, 0), (2, 0), (3, 0), (0, 0), (0, 1), (3, 1), (1, 1)]
-X_UNITS = [(0, 0), (3, 0), (2, 0), (0, 1), (1, 1), (3, 1), (2, 1), (1, 0)]
+D_UNITS = [(1, 1), (0, 1), (0, 0), (3, 1), (1, 0), (2, 1), (2, 0), (3, 0)]
+X_UNITS = [(2, 0), (2, 1), (1, 0), (3, 1), (1, 1), (3, 0), (0, 0), (0, 1)]
 CAST_ON = "SGGG"
-CAST_AHEAD = 2
-COPY_X = "SSSSSSSS"
-RES = "SSSSVSSS"
-LAG_QD, LAG_QX, LAG_X, LAG_O = 2, 2, 3, 1
-LOADS = "d1 g0 x0 d2 x2 d3 x3 d0 x1"
+CAST_AHEAD = 0
+COPY_X = "SSSSVVSV"
+RES = "SSSVSSVS"
+LAG_QD, LAG_QX, LAG_X, LAG_O = 2, 2, 2, 1
+LOADS = "d1 x2 g0 d0 x1 x3 d3 x0 d2"
 
 
 def tile_moe_bdw_lin_none_kernel(tc, xT, dyT, gate, offs, out):
@@ -73,6 +73,8 @@ def tile_moe_bdw_lin_none_kernel(tc, xT, dyT, gate, offs, out):
         gathered = {}
         grouped = {}
         pairs = {}
+        x_pairs = {}
+        x_ready = {}
         ready = {}
         done = set()
         count = {"acc": 0}
@@ -91,7 +93,7 @@ def tile_moe_bdw_lin_none_kernel(tc, xT, dyT, gate, offs, out):
 
         def gather_x(i):
             b, e = X_UNITS[i]
-            g = keep.tile([P, C], BF16, name=ring("gx", i, 0))
+            g = keep.tile([P, C], BF16, name=ring("gx", i, 2))
             view = g[:].rearrange("q (u p s) -> q p u s", u=2, s=2)
             nc.scalar.activation(view, x_bf[b][:].indirect(offsets_of(e)), COPY)
             gathered["X", i] = g
@@ -114,14 +116,16 @@ def tile_moe_bdw_lin_none_kernel(tc, xT, dyT, gate, offs, out):
             bank = psum.tile([P, 2, P], F32, name=ring("turnx", i, 2))
             for h in range(2):
                 nc.tensor.transpose(bank[:, h, :], g[:].bitcast(F32)[:, h * P : (h + 1) * P], ident[:])
-            gr = keep.tile([P, P * PACK], BF16, name=ring("grx", i, 0), align_bytes=64)
-            dst = gr[:].bitcast(F32).rearrange("p (k u) -> p k u", u=2)
+            b, e = X_UNITS[i]
+            if (b // 2, e) not in x_pairs:
+                x_pairs[b // 2, e] = keep.tile([P, 2, P * PACK], BF16, name=f"grx{b // 2}_{e}", align_bytes=64)
+            gr = x_pairs[b // 2, e][:, b % 2]
+            dst = gr.bitcast(F32).rearrange("p (k u) -> p k u", u=2)
             src = bank[:].rearrange("p u k -> p k u")
             if COPY_X[i] == "V":
                 nc.vector.tensor_copy(dst, src)
             else:
                 nc.scalar.copy(out=dst, in_=src)
-            grouped["X", i] = gr[:]
 
         def quantize_d(i):
             b, e = D_UNITS[i]
@@ -133,16 +137,25 @@ def tile_moe_bdw_lin_none_kernel(tc, xT, dyT, gate, offs, out):
                 scales=g_scales[e][:, cols],
                 in_=pairs[b // 2, e][:].rearrange("p h k t -> p (h k t)"),
             )
-            done.add(("D", b, e))
-            done.add(("D", b + 1 - 2 * (b % 2), e))
+            done.update([("D", b // 2 * 2, e), ("D", b // 2 * 2 + 1, e)])
 
         def quantize_x(i):
             b, e = X_UNITS[i]
-            cols = slice(b * P, (b + 1) * P)
+            pair = x_pairs[b // 2, e]
+            if X_UNITS[-1] in ((b // 2 * 2, e), (b // 2 * 2 + 1, e)):
+                halves = [b]
+            elif x_ready.setdefault((b // 2, e), b) == b:
+                return
+            else:
+                halves = [b // 2 * 2, b // 2 * 2 + 1]
+            first = halves[0]
+            cols = slice(first * P, (first + len(halves)) * P)
             nc.vector.quantize_mx(
-                out=x_codes[e][:, cols].bitcast(FP8X4), scales=x_scales[e][:, cols], in_=grouped["X", i]
+                out=x_codes[e][:, cols].bitcast(FP8X4),
+                scales=x_scales[e][:, cols],
+                in_=pair[:, first % 2 : first % 2 + len(halves)].rearrange("p h n -> p (h n)"),
             )
-            done.add(("X", b, e))
+            done.update([("X", half, e) for half in halves])
 
         def multiply(e, b, n0, width, engine):
             acc = psum.tile([P, N], F32, name=ring("acc", count["acc"], 3))
@@ -195,7 +208,7 @@ def tile_moe_bdw_lin_none_kernel(tc, xT, dyT, gate, offs, out):
                     need = [("X", b, e)] + [("D", q, e) for q in range(4)]
                     if (b, e) not in issued and all(v in done for v in need):
                         issued.append((b, e))
-                        if (b, e) == X_UNITS[-1] and True:
+                        if (b, e) == X_UNITS[-1] and False:
                             leaves = [multiply(e, b, 256 * q, 256, "SV"[q]) for q in range(2)]
                         else:
                             leaves = [multiply(e, b, 0, N, RES[len(issued) - 1])]

from contextlib import ExitStack

import concourse.mybir as mybir
from concourse.masks import make_identity

K, T, E, C, N = 512, 1024, 2, 512, 512
FLOPS = 2 * E * C * K * N
BYTES = 4 * (K * T + N * T + T + E * K * N) + 2 * 128 * (E * C // 16)

F32 = mybir.dt.float32
BF16 = mybir.dt.bfloat16
U32 = mybir.dt.uint32
U16 = mybir.dt.uint16
U8 = mybir.dt.uint8
FP8X4 = mybir.dt.float8_e4m3fn_x4
MULT = mybir.AluOpType.mult
ADD = mybir.AluOpType.add
COPY = mybir.ActivationFunctionType.Copy

P = 128
PACK = 4
D_UNITS = [(1, 1), (0, 1), (0, 0), (3, 1), (1, 0), (2, 1), (2, 0), (3, 0)]
X_UNITS = [(2, 0), (2, 1), (1, 0), (3, 1), (1, 1), (3, 0), (0, 0), (0, 1)]
CAST_ON = "SGGG"
CAST_AHEAD = 0
COPY_X = "SSSSVVSV"
RES = "SSSVSSVS"
LAG_QD, LAG_QX, LAG_X, LAG_O = 2, 2, 2, 1
LOADS = "d1 x2 g0 d0 x1 x3 d3 x0 d2"


def tile_moe_bdw_lin_none_kernel(tc, xT, dyT, gate, offs, out):
    nc = tc.nc
    with ExitStack() as ctx:
        keep = ctx.enter_context(tc.tile_pool(name="keep", bufs=1))
        psum = ctx.enter_context(tc.psum_pool(name="psum", bufs=1))

        offsets = keep.tile([P, E * C // 16], U16, name="offsets")
        nc.sync.dma_start(offsets[:], offs)
        dy = {}
        x = {}
        for name in LOADS.split():
            b = int(name[1])
            if name[0] == "g":
                gate_sb = keep.tile([P, E, PACK], F32, name="gate_sb")
                nc.sync.dma_start(gate_sb[:], gate[0:1, :].rearrange("o (e p t) -> p (o e) t", e=E, t=PACK))
            elif name[0] == "d":
                dy[b] = keep.tile([P, T], F32, name=f"dy{b}")
                nc.sync.dma_start(dy[b][:], dyT[b * P : (b + 1) * P, :])
            else:
                x[b] = keep.tile([P, T], F32, name=f"x{b}")
                nc.sync.dma_start(x[b][:], xT[b * P : (b + 1) * P, :])

        ident = keep.tile([P, P], F32, name="ident")
        make_identity(nc, ident[:])

        x_bf = {}

        def cast(b):
            x_bf[b] = keep.tile([P, T], BF16, name=f"xbf{b}")
            engine = CAST_ON[len(x_bf) - 1]
            if engine == "S":
                nc.scalar.copy(out=x_bf[b][:], in_=x[b][:])
            elif engine == "V":
                nc.vector.tensor_copy(x_bf[b][:], x[b][:])
            else:
                nc.gpsimd.tensor_scalar(x_bf[b][:], x[b][:], 1.0, 0.0, MULT, ADD)

        g_codes = [keep.tile([P, N], U32, name=f"gcodes{e}", align_bytes=64) for e in range(E)]
        g_scales = [keep.tile([P, N], U8, name=f"gscales{e}", align_bytes=64) for e in range(E)]
        x_codes = [keep.tile([P, K], U32, name=f"xcodes{e}", align_bytes=64) for e in range(E)]
        x_scales = [keep.tile([P, K], U8, name=f"xscales{e}", align_bytes=64) for e in range(E)]
        gathered = {}
        grouped = {}
        pairs = {}
        x_pairs = {}
        x_ready = {}
        ready = {}
        done = set()
        count = {"acc": 0}

        def offsets_of(e):
            return offsets[:, e * 32 : (e + 1) * 32]

        def ring(name, i, size):
            return f"{name}{i % size if size else i}"

        def gather_d(i):
            b, e = D_UNITS[i]
            g = keep.tile([P, C], F32, name=ring("gd", i, 0))
            nc.vector.tensor_copy(g[:], dy[b][:].indirect(offsets_of(e)))
            gathered["D", i] = g

        def gather_x(i):
            b, e = X_UNITS[i]
            g = keep.tile([P, C], BF16, name=ring("gx", i, 2))
            view = g[:].rearrange("q (u p s) -> q p u s", u=2, s=2)
            nc.scalar.activation(view, x_bf[b][:].indirect(offsets_of(e)), COPY)
            gathered["X", i] = g

        def turn_d(i):
            b, e = D_UNITS[i]
            g = gathered["D", i]
            bank = psum.tile([P, PACK, P], F32, name=ring("turnd", i, 3))
            for t in range(PACK):
                nc.tensor.transpose(bank[:, t, :], g[:, t::PACK], ident[:])
            if (b // 2, e) not in pairs:
                pairs[b // 2, e] = keep.tile([P, 2, P, PACK], BF16, name=f"grd{b // 2}_{e}", align_bytes=64)
            gr = pairs[b // 2, e][:, b % 2]
            nc.vector.tensor_tensor(
                gr, bank[:].rearrange("p t k -> p k t"), gate_sb[:, e : e + 1, :].to_broadcast([P, P, PACK]), MULT
            )

        def turn_x(i):
            g = gathered["X", i]
            bank = psum.tile([P, 2, P], F32, name=ring("turnx", i, 2))
            for h in range(2):
                nc.tensor.transpose(bank[:, h, :], g[:].bitcast(F32)[:, h * P : (h + 1) * P], ident[:])
            b, e = X_UNITS[i]
            if (b // 2, e) not in x_pairs:
                x_pairs[b // 2, e] = keep.tile([P, 2, P * PACK], BF16, name=f"grx{b // 2}_{e}", align_bytes=64)
            gr = x_pairs[b // 2, e][:, b % 2]
            dst = gr.bitcast(F32).rearrange("p (k u) -> p k u", u=2)
            src = bank[:].rearrange("p u k -> p k u")
            if COPY_X[i] == "V":
                nc.vector.tensor_copy(dst, src)
            else:
                nc.scalar.copy(out=dst, in_=src)

        def quantize_d(i):
            b, e = D_UNITS[i]
            if ready.setdefault((b // 2, e), b) == b:
                return
            cols = slice(b // 2 * 2 * P, (b // 2 + 1) * 2 * P)
            nc.vector.quantize_mx(
                out=g_codes[e][:, cols].bitcast(FP8X4),
                scales=g_scales[e][:, cols],
                in_=pairs[b // 2, e][:].rearrange("p h k t -> p (h k t)"),
            )
            done.update([("D", b // 2 * 2, e), ("D", b // 2 * 2 + 1, e)])

        def quantize_x(i):
            b, e = X_UNITS[i]
            pair = x_pairs[b // 2, e]
            if X_UNITS[-1] in ((b // 2 * 2, e), (b // 2 * 2 + 1, e)):
                halves = [b]
            elif x_ready.setdefault((b // 2, e), b) == b:
                return
            else:
                halves = [b // 2 * 2, b // 2 * 2 + 1]
            first = halves[0]
            cols = slice(first * P, (first + len(halves)) * P)
            nc.vector.quantize_mx(
                out=x_codes[e][:, cols].bitcast(FP8X4),
                scales=x_scales[e][:, cols],
                in_=pair[:, first % 2 : first % 2 + len(halves)].rearrange("p h n -> p (h n)"),
            )
            done.update([("X", half, e) for half in halves])

        def multiply(e, b, n0, width, engine):
            acc = psum.tile([P, N], F32, name=ring("acc", count["acc"], 3))
            count["acc"] += 1
            k = slice(b * P, (b + 1) * P)
            n = slice(n0, n0 + width)
            nc.tensor.matmul_mx(
                out=acc[:, 0:width],
                lhsT=x_codes[e][:, k].bitcast(FP8X4),
                lhsT_scale=x_scales[e][:, k],
                rhs=g_codes[e][:, n].bitcast(FP8X4),
                rhs_scale=g_scales[e][:, n],
                start=True,
                stop=True,
            )

            def leave():
                res = keep.tile([P, width], F32, name=f"res{e}_{b}_{n0}")
                if engine == "S":
                    nc.scalar.copy(out=res[:], in_=acc[:, 0:width])
                else:
                    nc.vector.tensor_copy(out=res[:], in_=acc[:, 0:width])
                nc.sync.dma_start(out[e, k, n], res[:])

            return leave

        issued = []
        pending = []
        for i in range(8 + LAG_X + max(LAG_QD, LAG_QX) + LAG_O + 2):
            for ahead in range(min(i - LAG_X + CAST_AHEAD + 1, 8)):
                if X_UNITS[ahead][0] not in x_bf:
                    cast(X_UNITS[ahead][0])
            if i < 8:
                gather_d(i)
            j = i - LAG_X
            if 0 <= j < 8:
                gather_x(j)
            if 0 <= i - 1 < 8:
                turn_d(i - 1)
            if 0 <= j - 1 < 8:
                turn_x(j - 1)
            for at, leave in [p for p in pending if p[0] == i]:
                leave()
            if 0 <= i - LAG_QD < 8:
                quantize_d(i - LAG_QD)
            if 0 <= j - LAG_QX < 8:
                quantize_x(j - LAG_QX)
            for e in range(E):
                for b in range(4):
                    need = [("X", b, e)] + [("D", q, e) for q in range(4)]
                    if (b, e) not in issued and all(v in done for v in need):
                        issued.append((b, e))
                        if (b, e) == X_UNITS[-1] and False:
                            leaves = [multiply(e, b, 256 * q, 256, "SV"[q]) for q in range(2)]
                        else:
                            leaves = [multiply(e, b, 0, N, RES[len(issued) - 1])]
                        if LAG_O == 0:
                            for leave in leaves:
                                leave()
                        else:
                            pending.extend([(i + LAG_O, leave) for leave in leaves])
